import numpy as np, ml_dtypes
CORES = [3,5,19,21,35,37,51,53,67,69]
N = 10
import mx_ref
NC = 256
BF = ml_dtypes.bfloat16
def setup_inputs(rng):
    def f(*shape):
        return mx_ref.flush((rng.standard_normal(shape, dtype=np.float32) * np.exp2(rng.integers(-2, 3, shape[:-1] + (1,)))).astype(BF))
    return {"x": f(N, 128, 512), "w": f(N, 128, 4 * NC)}
def setup_inputs_blocks(rng):
    d = setup_inputs(rng)
    for k in ("x", "w"): d[k] = mx_ref.spread(d[k], rng, 4)
    return d
def setup_inputs_wide(rng):
    d = setup_inputs(rng)
    for k in ("x", "w"): d[k] = mx_ref.flush((d[k].astype(np.float32) * np.exp2(rng.integers(-6, 7, (N, 1, 1))).astype(np.float32)).astype(BF))
    return d
def setup_inputs_near(rng):
    d = setup_inputs(rng); v = d["w"].astype(np.float32).reshape(N, 128, -1, 4)
    d["w"] = mx_ref.flush((v[:1, :, :1] + v / 64).reshape(d["w"].shape).astype(BF))
    return d
def setup_inputs_twins(rng):
    d = setup_inputs(rng); v = d["w"].reshape(N, 128, -1, 4).copy(); a, b = rng.permutation(N)[:2]; i, j, k = rng.integers(0, v.shape[2], 3)
    v[a, :, i] = (v[a, :, i].astype(np.float32) * 8).astype(BF); v[a, :, j] = v[a, :, i]; v[b, :, k] = v[a, :, i]
    d["w"] = v.reshape(d["w"].shape)
    return d
def reference(x, w):
    W = [mx_ref.quantize(w[r]) for r in range(N)]
    y = np.zeros((N, 128, 2), np.float32)
    for j in range(N):
        X = mx_ref.quantize(x[j])
        L = np.concatenate([mx_ref.matmul(X, W[r]) for r in range(N)], axis=1)
        y[j][:, 0] = L.max(axis=1); y[j][:, 1] = L.argmax(axis=1)
    return {"y": y}

from concourse.bass import DstId, RemoteDMATransfer
from concourse.mybir import dt, AluOpType, AxisListType, ActivationFunctionType

N = 10
CHIPS = 5
TOK = 128
NC = 256
BANK = 512
LOW = -1e29

SCRATCH = {
    "xt": ("sbuf", [128, 4 * TOK], "bfloat16"),
    "wt": ("sbuf", [128, 4 * NC], "bfloat16"),
    "xq": ("sbuf", [128, TOK], "float8_e4m3fn_x4"),
    "xs": ("sbuf", [128, TOK], "uint8"),
    "wq": ("sbuf", [128, 2 * NC], "float8_e4m3fn_x4"),
    "ws": ("sbuf", [128, 2 * NC], "uint8"),
    "fq": ("sbuf", [128, CHIPS * TOK], "float8_e4m3fn_x4"),
    "fs": ("sbuf", [128, CHIPS * TOK], "uint8"),
    "low": ("sbuf", [128, NC], "float32"),
    "run0": ("sbuf", [128, 4 * NC], "float32"),
    "run1": ("sbuf", [128, 4 * NC], "float32"),
    "run2": ("sbuf", [128, 4 * NC], "float32"),
    "run3": ("sbuf", [128, 4 * NC], "float32"),
    "run4": ("sbuf", [128, 4 * NC], "float32"),
    "cand": ("sbuf", [128, 2 * N], "float32"),
    "base": ("sbuf", [128, N], "float32"),
    "gidx": ("sbuf", [128, N], "float32"),
    "below": ("sbuf", [128, N], "float32"),
    "yt": ("sbuf", [128, 2 * N], "float32"),
    "ps": ("psum", [128, 8 * BANK], "float32"),
}
SEMAPHORES = ["ldx", "ldw", "q", "loc", "xa0", "xa1", "xa2", "xa3", "xa4", "wa", "mm", "sc", "ct", "res", "st", "bs",
              "fill", "fin", "own"]


def engines(mask):
    return bin(mask).count("1")


def rank_program(g, core, T, topo):
    rank = T.rank_of(core)
    if rank is None:
        return
    cores = list(T.cores)
    S = T.sem
    chips = []
    for c in cores:
        if topo.chip(c) not in chips:
            chips.append(topo.chip(c))
    C = len(chips)
    me = chips.index(topo.chip(core))
    here = [r for r in range(N) if topo.chip(cores[r]) == topo.chip(core)]
    mine = here.index(rank)
    other = 1 - mine
    peer = cores[here[other]]
    line = [[c for c in cores if topo.chip(c) == ch and topo.die(c) == topo.die(core)][0] for ch in chips]
    to = [line[(me + d) % C] for d in range(1, C)]
    frm = [(me - d) % C for d in range(C)]
    far = topo.mask(core, to[0])
    near = topo.mask(core, peer) & ~far
    nf, nn = engines(far), engines(near)

    def dst_id(c):
        rid, pid, _ = topo.addr(c)
        return DstId(rid=rid, pnc=pid)

    def block(buf, i):
        return buf[:, i * TOK:(i + 1) * TOK]

    def half(buf, h):
        return buf[:, h * NC:(h + 1) * NC]

    g.sync.dma_start(T.xt[:], T.x[:]).then_inc(S.ldx, 16)
    g.sync.dma_start(T.wt[:], T.w[:]).then_inc(S.ldw, 16)

    prods = [(0, mine)]
    for d in range(1, C):
        prods += [(d, mine), (d, other)]
    prods.append((0, other))
    run = [T["run%d" % d] for d in range(C)]
    last = 4 * (NC - 1)

    def lane(h):
        return 0 if h == 1 else 2

    g.vector.memset(T.low[:], LOW).then_inc(S.fill, 1)
    g.vector.wait_ge(S.ldx, 16)
    g.vector.quantize_mx(T.xq[:], T.xs[:], T.xt[:]).then_inc(S.q, 1)
    g.vector.wait_ge(S.ldw, 16)
    g.vector.quantize_mx(half(T.wq, mine), half(T.ws, mine), T.wt[:]).then_inc(S.q, 1)

    g.iota(T.base[:], [[-NC, N]], (N - 1) * NC, 0, allow_small_or_imprecise_dtypes=True).then_inc(S.bs, 1)
    g.wait_ge(S.q, 1)
    for src, dst in ((T.xs[:], block(T.fs, me)),
                     (T.xq[:].bitcast(dt.uint8), block(T.fq, me).bitcast(dt.uint8))):
        g.remote_dma_fused([RemoteDMATransfer(
            dst_ids=[dst_id(c) for c in to], dma_engine_mask=far, remote_sem=S["xa%d" % me],
            srcs=[src], dsts=[dst] * len(to))], local_sem=S.loc)
    g.wait_ge(S.q, 2)
    rid, pid, _ = topo.addr(peer)
    g.remote_dma(half(T.wq, mine).bitcast(dt.uint8), half(T.wq, mine).bitcast(dt.uint8), S.wa, S.loc, pid, rid, near)
    g.remote_dma(half(T.ws, mine), half(T.ws, mine), S.wa, S.loc, pid, rid, near)

    g.tensor.wait_ge(S.q, 2)
    have_w = False
    seen = {0}
    for i, (d, h) in enumerate(prods):
        if d not in seen:
            seen.add(d)
            g.tensor.wait_ge(S["xa%d" % frm[d]], 2 * nf)
        if h == other and not have_w:
            have_w = True
            g.tensor.wait_ge(S.wa, 2 * nn)
        if i >= 8:
            g.tensor.wait_ge(S.sc, i - 8 + 1)
        b = i % 8
        lq, ls = (T.xq[:], T.xs[:]) if d == 0 else (block(T.fq, frm[d]), block(T.fs, frm[d]))
        g.tensor.matmul_mx(T.ps[:, b * BANK:b * BANK + NC], lq, ls, half(T.wq, h), half(T.ws, h), True, True).then_inc(S.mm, 1)

    g.vector.wait_ge(S.fill, 1)
    for i, (d, h) in enumerate(prods):
        g.vector.wait_ge(S.mm, i + 1)
        b = i % 8
        g.vector.tensor_tensor_scan(run[d][:, lane(h):4 * NC:4], T.ps[:, b * BANK:b * BANK + NC], T.low[:], LOW,
                                    AluOpType.max, AluOpType.max).then_inc(S.sc, 1)

    for i, (d, h) in enumerate(prods):
        l = lane(h)
        g.scalar.wait_ge(S.sc, i + 1)
        v = run[d][:, l:last:4]
        g.scalar.activation(v, v, ActivationFunctionType.Sign, bias=run[d][:, last + l:last + l + 1], scale=-1.0,
                            accum_out=run[d][:, last + l + 1:last + l + 2]).then_inc(S.ct, 1)

    slot = 4 * (C - 1 - me)
    for d in range(1, C):
        g.wait_ge(S.ct, prods.index((d, other)) + 1)
        rid, pid, _ = topo.addr(line[frm[d]])
        g.remote_dma(T.cand[:, slot:slot + 4], run[d][:, last:last + 4], S.res, S.loc, pid, rid, far)

    g.vector.wait_ge(S.ct, len(prods))
    g.vector.tensor_copy(T.cand[:, slot:slot + 4], run[0][:, last:last + 4]).then_inc(S.own, 1)
    g.vector.wait_ge(S.bs, 1)
    g.vector.wait_ge(S.own, 1)
    g.vector.wait_ge(S.res, (C - 1) * nf)
    vals, cnts = T.cand[:, 0:2 * N:2], T.cand[:, 1:2 * N:2]
    top = T.yt[:, 2 * N - 2:2 * N - 1]
    g.vector.tensor_reduce(top, vals, AxisListType.X, AluOpType.max).then_inc(S.fin, 1)
    g.vector.tensor_tensor(T.gidx[:], cnts, T.base[:], AluOpType.add).then_inc(S.fin, 1)
    g.vector.wait_ge(S.fin, 2)
    g.vector.tensor_scalar(T.below[:], vals, top, None, AluOpType.is_lt).then_inc(S.fin, 1)
    g.vector.wait_ge(S.fin, 3)
    g.vector.tensor_tensor_scan(T.yt[:, 1:2 * N:2], T.below[:], T.gidx[:], 0.0, AluOpType.mult, AluOpType.max).then_inc(S.fin, 1)

    g.sync.wait_ge(S.fin, 4)
    g.sync.dma_start(T.y[:], T.yt[:, 2 * N - 2:2 * N]).then_inc(S.st, 16)
    g.sync.wait_ge(S.st, 16)
    g.wait_ge(S.loc, 2 * nf + 2 * nn + (C - 1) * nf)
